import numpy as np
import ml_dtypes


def mxq(x, axis, fmt="e4m3"):
    dtype, down = {"e4m3": (ml_dtypes.float8_e4m3fn, 7), "e5m2": (ml_dtypes.float8_e5m2, 14)}[fmt]
    v = np.moveaxis(np.asarray(x, np.float32).astype(ml_dtypes.bfloat16).astype(np.float64), axis, -1)
    blocks = v.reshape(v.shape[:-1] + (-1, 32))
    amax = np.abs(blocks).max(-1, keepdims=True)
    byte = np.maximum(np.where(amax > 0, np.frexp(amax)[1] - 1 + 127, 0) - down, 1)
    scale = np.exp2(byte - 127.0)
    codes = (blocks / scale).astype(np.float32).astype(dtype).astype(np.float64)
    return np.moveaxis((codes * scale).reshape(v.shape), -1, axis)


WIDE = False


def mx_kscale(k):
    if not WIDE:
        return np.ones(k)
    levels = np.array([10, -10, 5, -5, 0])
    if k % 512:
        return np.exp2(np.random.permutation(np.resize(levels, k // 32))).repeat(32)
    a = np.empty((k // 512, 16))
    for p in range(k // 512):
        a[p, :8] = np.random.permutation(np.resize(levels, 8))
        for g in range(8):
            far = levels[np.abs(levels - a[p, g]) >= 10]
            a[p, g + 8] = far[np.random.randint(len(far))]
    return np.exp2(a.ravel()).repeat(32)


def f64(x):
    return np.asarray(x).astype(np.float64)


def striped8(idx):
    return np.concatenate([x.reshape(-1, 16).T for x in idx]).astype(np.uint16)


def runs(offs, k):
    lists = np.stack([offs[16 * r : 16 * r + 16].T.reshape(-1) for r in range(8)]).astype(np.int64)
    return lists[np.arange(k) % 512 // 64]


def pack_weight(w):
    k, n = w.shape
    w = f64(np.asarray(w, np.float32).astype(ml_dtypes.bfloat16)).reshape(k // 32, 32, n)
    amax = np.abs(w).max(1)
    byte = np.clip(np.where(amax > 0, np.frexp(amax)[1] - 1 + 127 - 7, 1), 1, 254)
    scaled = (w * np.exp2(127.0 - byte)[:, None, :]).reshape(k, n).astype(np.float32)
    words = np.ascontiguousarray(scaled.reshape(k // 512, 128, 4, n).transpose(0, 1, 3, 2)).astype(ml_dtypes.float8_e4m3fn).view(np.uint8)
    return words, np.ascontiguousarray(byte.astype(np.uint8).reshape(k // 512, 16, n))


def unpack_weight(words, scales):
    g, p, n, _ = words.shape
    vals = np.ascontiguousarray(words).view(ml_dtypes.float8_e4m3fn).astype(np.float64) * np.repeat(np.exp2(scales.astype(np.float64) - 127.0), 8, axis=1)[..., None]
    return vals.transpose(0, 1, 3, 2).reshape(g * 512, n)


def sigmoid(v):
    return 1.0 / (1.0 + np.exp(-np.maximum(v, -700.0)))


K, T, S, H, C = 512, 2048, 512, 512, 512


def setup_inputs():
    n = np.random.standard_normal
    s = mx_kscale(K)[:, None]
    packed_xT = pack_weight(n((K, T)) * s)
    return {
        "x_words": packed_xT[0],
        "x_scales": packed_xT[1],
        "w1": (n((K, H)) / np.sqrt(K) / s).astype(np.float32),
        "gs": (np.random.uniform(0.5, 1.5, (K, 1)) / s).astype(np.float32),
        "offs": striped8(np.random.randint(0, T, (8, S))),
        "n1": striped8(np.stack([np.random.permutation(S) for _ in range(8)])),
        "n2": striped8(np.stack([np.random.permutation(S) for _ in range(8)])),
        "n3": striped8(np.stack([np.random.permutation(S) for _ in range(8)])),
        "cand": striped8(np.random.randint(0, T, (8, C))),
        "n4": striped8(np.stack([np.random.permutation(S) for _ in range(8)])),
        "n5": striped8(np.stack([np.random.permutation(S) for _ in range(8)])),
    }


def reference(x_words, x_scales, w1, gs, offs, n1, n2, n3, cand, n4, n5):
    x_cand = unpack_weight(x_words, x_scales)[np.arange(K)[:, None], runs(cand, K)]
    xq = unpack_weight(x_words, x_scales)[np.arange(K)[:, None], runs(offs, K)]
    y = mxq(f64(w1), 0, "e4m3").T @ xq
    pa = y[np.arange(H)[:, None], runs(n1, H)]
    z = f64(gs) * (pa + (sigmoid(y[np.arange(H)[:, None], runs(n2, H)])) * (y[np.arange(H)[:, None], runs(n3, H)] - pa))
    s = 0.0625 * ((x_cand.T @ mxq(z, 0, "e4m3")))
    return s * (s[np.arange(C)[:, None], runs(n4, C)] - (s[np.arange(C)[:, None], runs(n5, C)]))

@@ -1,0 +1,183 @@
+from contextlib import ExitStack
+
+import concourse.mybir as mybir
+
+K, T, S, H, C = 512, 2048, 512, 512, 512
+FLOPS = 2 * K * H * S + 2 * H * C * S
+
+F32 = mybir.dt.float32
+BF16 = mybir.dt.bfloat16
+I32 = mybir.dt.int32
+U32 = mybir.dt.uint32
+U16 = mybir.dt.uint16
+U8 = mybir.dt.uint8
+FP8X4 = mybir.dt.float8_e4m3fn_x4
+ALU = mybir.AluOpType
+ACT = mybir.ActivationFunctionType
+
+P = 128
+PACK = 4
+WINDOW = 1024
+SCORE_SCALE = 0.0625
+
+
+def tile_picked_hcandlerpwind_none_p_kernel(
+    tc, x_words, x_scales, w1, gs, offs, n1, n2, n3, cand, n4, n5, out
+):
+    nc = tc.nc
+    with ExitStack() as ctx:
+        lists = ctx.enter_context(tc.tile_pool(name="lists", bufs=1))
+        keep = ctx.enter_context(tc.tile_pool(name="keep", bufs=1))
+        psum = ctx.enter_context(tc.psum_pool(name="psum", bufs=1))
+
+        def load_list(name, dram):
+            offsets = lists.tile([P, S // 16], U16, name=name)
+            nc.sync.dma_start(offsets[:], dram)
+            return offsets
+
+        table_scales = keep.tile([P, T], U8, align_bytes=64)
+        nc.vector.memset(table_scales[:].bitcast(I32), 0)
+        place_plane = keep.tile([P, S], U8, align_bytes=64)
+        cand_plane = keep.tile([P, C], U8, align_bytes=64)
+        nc.vector.memset(place_plane[:].bitcast(I32), 0)
+        nc.vector.memset(cand_plane[:].bitcast(I32), 0)
+
+        offs_sb = load_list("offs_sb", offs)
+        nc.scalar.dma_start(table_scales[0:P:8, :].bitcast(I32), x_scales[0].bitcast(I32))
+        cand_sb = load_list("cand_sb", cand)
+        w_rows = w1.rearrange("(p j) c -> p j c", j=PACK)
+        w_raw = []
+        half = H // 2
+        w_raw.append(keep.tile([P, PACK, half], F32, name="w_raw0"))
+        nc.sync.dma_start(w_raw[0][:], w_rows[:, :, 0:half])
+        n2_sb = load_list("n2_sb", n2)
+        n3_sb = load_list("n3_sb", n3)
+        n1_sb = load_list("n1_sb", n1)
+        w_raw.append(keep.tile([P, PACK, half], F32, name="w_raw1"))
+        nc.sync.dma_start(w_raw[1][:], w_rows[:, :, half:H])
+        table_words = keep.tile([P, T], U32, align_bytes=64)
+        nc.sync.dma_start(table_words[:].bitcast(I32), x_words[0].rearrange("p c r -> p (c r)").bitcast(I32))
+        n4_sb = load_list("n4_sb", n4)
+        n5_sb = load_list("n5_sb", n5)
+        gain = keep.tile([P, PACK], F32)
+        nc.gpsimd.dma_start(gain[:], gs.rearrange("(p t) o -> p (t o)", t=PACK))
+        neg_gain = keep.tile([P, PACK], F32)
+        nc.gpsimd.tensor_scalar(neg_gain[:], gain[:], -1.0, 0.0, ALU.mult, ALU.add)
+
+        warm = keep.tile([P, 1], F32)
+        nc.gpsimd.memset(warm[:], 0.0)
+        warm_out = keep.tile([P, 1], F32)
+        nc.scalar.activation(warm_out[:], warm[:], ACT.Sigmoid)
+
+        def move_scale_rows(plane, picked):
+            for j in range(4):
+                nc.sync.dma_start(plane[j:P:32, :].bitcast(I32), picked[8 * j : P : 32, :].bitcast(I32))
+
+        place_bytes = keep.tile([P, S], U8, align_bytes=64)
+        nc.vector.tensor_copy(place_bytes[:], table_scales[:].indirect(offs_sb[:]))
+        move_scale_rows(place_plane, place_bytes)
+
+        w_bf = keep.tile([P, PACK, P, PACK], BF16, align_bytes=64)
+        for h in range(2):
+            nc.scalar.copy(
+                w_bf[:, :, 64 * h : 64 * (h + 1), :].rearrange("p t m j -> p m j t"),
+                w_raw[h][:].rearrange("p j (m t) -> p m j t", t=PACK),
+            )
+
+        cand_bytes = keep.tile([P, C], U8, align_bytes=64)
+        nc.vector.tensor_copy(cand_bytes[:], table_scales[:].indirect(cand_sb[:]))
+        cand_bytes_dealt = keep.tile([P, C], U8, align_bytes=64)
+        nc.vector.tensor_copy(
+            cand_bytes_dealt[:].bitcast(I32).rearrange("p (t u) -> p u t", t=PACK),
+            cand_bytes[:].bitcast(I32).rearrange("p (u t) -> p u t", t=PACK),
+        )
+        move_scale_rows(cand_plane, cand_bytes_dealt)
+
+        w_codes = keep.tile([P, H], U32, align_bytes=64)
+        w_scales = keep.tile([P, H], U8, align_bytes=64)
+        nc.vector.quantize_mx(
+            out=w_codes[:].bitcast(FP8X4), scales=w_scales[:], in_=w_bf[:].rearrange("p t m j -> p (t m j)")
+        )
+        place_words = keep.tile([P, S], U32, align_bytes=64)
+        nc.vector.tensor_copy(place_words[:], table_words[:].indirect(offs_sb[:]))
+
+        banks = [psum.tile([P, S], F32, name="y_bank%d" % t) for t in range(PACK)]
+        for t in range(PACK):
+            cols = slice(P * t, P * (t + 1))
+            nc.tensor.matmul_mx(
+                out=banks[t][:],
+                lhsT=w_codes[:, cols].bitcast(FP8X4),
+                lhsT_scale=w_scales[:, cols],
+                rhs=place_words[:].bitcast(FP8X4),
+                rhs_scale=place_plane[:],
+                start=True,
+                stop=True,
+            )
+
+        cand_words = keep.tile([P, C], U32, align_bytes=64)
+        nc.vector.tensor_copy(cand_words[:], table_words[:].indirect(cand_sb[:]))
+        cand_words_dealt = keep.tile([P, C], U32, align_bytes=64)
+        nc.vector.tensor_copy(
+            cand_words_dealt[:].rearrange("p (t u e) -> p u t e", t=PACK, e=4),
+            cand_words[:].rearrange("p (u t e) -> p u t e", t=PACK, e=4),
+        )
+
+        from_n1 = keep.tile([P, PACK, S], F32)
+        from_n3 = keep.tile([P, PACK, S], F32)
+        for t in range(PACK):
+            y = keep.tile([P, WINDOW], F32, name="y%d" % t)
+            nc.scalar.copy(y[:, 0:S], banks[t][:])
+            gate = keep.tile([P, S], F32, name="gate%d" % t)
+            nc.scalar.activation(gate[:], y[:].indirect(n2_sb[:]), ACT.Sigmoid)
+            w3 = keep.tile([P, S], F32, name="w3_%d" % t)
+            nc.scalar.activation(w3[:], gate[:], ACT.Copy, scale=gain[:, t : t + 1])
+            w1g = keep.tile([P, S], F32, name="w1g_%d" % t)
+            nc.scalar.activation(w1g[:], gate[:], ACT.Identity, scale=neg_gain[:, t : t + 1], bias=gain[:, t : t + 1])
+            nc.vector.tensor_tensor(from_n3[:, t, :], y[:].indirect(n3_sb[:]), w3[:], ALU.mult)
+            nc.vector.tensor_tensor(from_n1[:, t, :], y[:].indirect(n1_sb[:]), w1g[:], ALU.mult)
+
+        z_bf = keep.tile([P, S, PACK], BF16, align_bytes=64)
+        z_codes = keep.tile([P, S], U32, align_bytes=64)
+        z_scales = keep.tile([P, S], U8, align_bytes=64)
+        s_banks = [[psum.tile([P, S // 2], F32, name="s_bank%d" % t, tag="s%d" % t) for t in range(PACK)]]
+        s_banks.append([psum.tile([P, S // 2], F32, name="s_bankb%d" % t, tag="y_bank%d" % t) for t in range(PACK)])
+        s_tiles = [keep.tile([P, WINDOW], F32, name="s%d" % t) for t in range(PACK)]
+        for h in range(2):
+            cols = slice(256 * h, 256 * (h + 1))
+            nc.vector.tensor_tensor(
+                z_bf[:, cols, :].rearrange("p (c i) t -> p c t i", i=4),
+                from_n1[:, :, cols].rearrange("p t (c i) -> p c t i", i=4),
+                from_n3[:, :, cols].rearrange("p t (c i) -> p c t i", i=4),
+                ALU.add,
+            )
+        for h in range(2):
+            cols = slice(256 * h, 256 * (h + 1))
+            nc.vector.quantize_mx(
+                out=z_codes[:, cols].bitcast(FP8X4),
+                scales=z_scales[:, cols],
+                in_=z_bf[:, cols, :].rearrange("p c t -> p (c t)"),
+            )
+            for t in range(PACK):
+                rows = slice(P * t, P * (t + 1))
+                nc.tensor.matmul_mx(
+                    out=s_banks[h][t][:],
+                    lhsT=cand_words_dealt[:, rows].bitcast(FP8X4),
+                    lhsT_scale=cand_plane[:, rows],
+                    rhs=z_codes[:, cols].bitcast(FP8X4),
+                    rhs_scale=z_scales[:, cols],
+                    start=True,
+                    stop=True,
+                )
+            for t in range(PACK):
+                nc.scalar.activation(s_tiles[t][:, cols], s_banks[h][t][:], ACT.Copy, scale=SCORE_SCALE)
+
+        out_rows = out.rearrange("(u t e) c -> t u e c", t=PACK, e=4)
+        for t in range(PACK):
+            s = s_tiles[t]
+            at_n5 = keep.tile([P, S], F32, name="at_n5_%d" % t)
+            nc.vector.tensor_copy(at_n5[:], s[:].indirect(n5_sb[:]))
+            diff = keep.tile([P, S], F32, name="diff%d" % t)
+            nc.vector.tensor_tensor(diff[:], s[:].indirect(n4_sb[:]), at_n5[:], ALU.subtract)
+            res = keep.tile([P, S], F32, name="res%d" % t)
+            nc.vector.tensor_tensor(res[:], diff[:], s[:, 0:S], ALU.mult)
+            nc.sync.dma_start(out_rows[t], res[:])

@@ -1,6 +1,7 @@
 from contextlib import ExitStack
 
 import concourse.mybir as mybir
+from concourse.masks import make_identity
 
 K, T, S, H, C = 512, 2048, 512, 512, 512
 FLOPS = 2 * K * H * S + 2 * H * C * S
@@ -19,6 +20,7 @@ P = 128
 PACK = 4
 WINDOW = 1024
 SCORE_SCALE = 0.0625
+Z_CHUNKS = [(0, 256), (256, 384), (384, 512)]
 
 
 def tile_picked_hcandlerpwind_none_p_kernel(
@@ -35,26 +37,27 @@ def tile_picked_hcandlerpwind_none_p_kernel(
             nc.sync.dma_start(offsets[:], dram)
             return offsets
 
+        def bank(number, width, name):
+            return psum.tile([P, width], F32, name=name, tag="bank%d" % number)
+
         table_scales = keep.tile([P, T], U8, align_bytes=64)
-        nc.vector.memset(table_scales[:].bitcast(I32), 0)
+        nc.gpsimd.memset(table_scales[:].bitcast(I32), 0)
         place_plane = keep.tile([P, S], U8, align_bytes=64)
         cand_plane = keep.tile([P, C], U8, align_bytes=64)
-        nc.vector.memset(place_plane[:].bitcast(I32), 0)
-        nc.vector.memset(cand_plane[:].bitcast(I32), 0)
+        nc.gpsimd.memset(place_plane[:].bitcast(I32), 0)
+        nc.gpsimd.memset(cand_plane[:].bitcast(I32), 0)
 
         offs_sb = load_list("offs_sb", offs)
-        nc.scalar.dma_start(table_scales[0:P:8, :].bitcast(I32), x_scales[0].bitcast(I32))
-        cand_sb = load_list("cand_sb", cand)
+        nc.sync.dma_start(table_scales[0:P:8, :].bitcast(I32), x_scales[0].bitcast(I32))
         w_rows = w1.rearrange("(p j) c -> p j c", j=PACK)
-        w_raw = []
         half = H // 2
-        w_raw.append(keep.tile([P, PACK, half], F32, name="w_raw0"))
-        nc.sync.dma_start(w_raw[0][:], w_rows[:, :, 0:half])
+        w_raw = [keep.tile([P, PACK, half], F32, name="w_raw%d" % h) for h in range(2)]
+        for h in range(2):
+            nc.sync.dma_start(w_raw[h][:], w_rows[:, :, half * h : half * (h + 1)])
+        cand_sb = load_list("cand_sb", cand)
         n2_sb = load_list("n2_sb", n2)
         n3_sb = load_list("n3_sb", n3)
         n1_sb = load_list("n1_sb", n1)
-        w_raw.append(keep.tile([P, PACK, half], F32, name="w_raw1"))
-        nc.sync.dma_start(w_raw[1][:], w_rows[:, :, half:H])
         table_words = keep.tile([P, T], U32, align_bytes=64)
         nc.sync.dma_start(table_words[:].bitcast(I32), x_words[0].rearrange("p c r -> p (c r)").bitcast(I32))
         n4_sb = load_list("n4_sb", n4)
@@ -65,9 +68,11 @@ def tile_picked_hcandlerpwind_none_p_kernel(
         nc.gpsimd.tensor_scalar(neg_gain[:], gain[:], -1.0, 0.0, ALU.mult, ALU.add)
 
         warm = keep.tile([P, 1], F32)
-        nc.gpsimd.memset(warm[:], 0.0)
+        nc.vector.memset(warm[:], 0.0)
         warm_out = keep.tile([P, 1], F32)
         nc.scalar.activation(warm_out[:], warm[:], ACT.Sigmoid)
+        ident = keep.tile([P, P], F32)
+        make_identity(nc, ident[:])
 
         def move_scale_rows(plane, picked):
             for j in range(4):
@@ -99,20 +104,29 @@ def tile_picked_hcandlerpwind_none_p_kernel(
             out=w_codes[:].bitcast(FP8X4), scales=w_scales[:], in_=w_bf[:].rearrange("p t m j -> p (t m j)")
         )
         place_words = keep.tile([P, S], U32, align_bytes=64)
-        nc.vector.tensor_copy(place_words[:], table_words[:].indirect(offs_sb[:]))
+        for h in range(2):
+            nc.vector.tensor_copy(
+                place_words[:, 256 * h : 256 * (h + 1)], table_words[:].indirect(offs_sb[:, 16 * h : 16 * (h + 1)])
+            )
 
-        banks = [psum.tile([P, S], F32, name="y_bank%d" % t) for t in range(PACK)]
-        for t in range(PACK):
-            cols = slice(P * t, P * (t + 1))
+        def project(dst, t, cols):
+            rows = slice(P * t, P * (t + 1))
             nc.tensor.matmul_mx(
-                out=banks[t][:],
-                lhsT=w_codes[:, cols].bitcast(FP8X4),
-                lhsT_scale=w_scales[:, cols],
-                rhs=place_words[:].bitcast(FP8X4),
-                rhs_scale=place_plane[:],
+                out=dst,
+                lhsT=w_codes[:, rows].bitcast(FP8X4),
+                lhsT_scale=w_scales[:, rows],
+                rhs=place_words[:, cols].bitcast(FP8X4),
+                rhs_scale=place_plane[:, cols],
                 start=True,
                 stop=True,
             )
+
+        y0_banks = [bank(4 * h, 256, "y0_bank%d" % h) for h in range(2)]
+        for h in range(2):
+            project(y0_banks[h][:], 0, slice(256 * h, 256 * (h + 1)))
+        y_banks = [bank(t, S, "y_bank%d" % t) for t in range(1, PACK)]
+        for t in range(1, PACK):
+            project(y_banks[t - 1][:], t, slice(0, S))
 
         cand_words = keep.tile([P, C], U32, align_bytes=64)
         nc.vector.tensor_copy(cand_words[:], table_words[:].indirect(cand_sb[:]))
@@ -122,62 +136,114 @@ def tile_picked_hcandlerpwind_none_p_kernel(
             cand_words[:].rearrange("p (u t e) -> p u t e", t=PACK, e=4),
         )
 
+        y_tiles = [keep.tile([P, WINDOW], F32, name="y%d" % t) for t in range(PACK - 1)]
+        for h in range(2):
+            nc.scalar.copy(y_tiles[0][:, 256 * h : 256 * (h + 1)], y0_banks[h][:])
+        for t in range(1, PACK - 1):
+            nc.vector.tensor_copy(y_tiles[t][:, 0:S], y_banks[t - 1][:])
         from_n1 = keep.tile([P, PACK, S], F32)
         from_n3 = keep.tile([P, PACK, S], F32)
         for t in range(PACK):
-            y = keep.tile([P, WINDOW], F32, name="y%d" % t)
-            nc.scalar.copy(y[:, 0:S], banks[t][:])
+            y = y_tiles[t]
             gate = keep.tile([P, S], F32, name="gate%d" % t)
-            nc.scalar.activation(gate[:], y[:].indirect(n2_sb[:]), ACT.Sigmoid)
+            for h in range(2):
+                nc.scalar.activation(gate[:, 256 * h : 256 * (h + 1)], y[:].indirect(n2_sb[:, 16 * h : 16 * (h + 1)]), ACT.Sigmoid)
             w3 = keep.tile([P, S], F32, name="w3_%d" % t)
-            nc.scalar.activation(w3[:], gate[:], ACT.Copy, scale=gain[:, t : t + 1])
+            for h in range(2):
+                cols = slice(256 * h, 256 * (h + 1))
+                nc.scalar.activation(w3[:, cols], gate[:, cols], ACT.Copy, scale=gain[:, t : t + 1])
             w1g = keep.tile([P, S], F32, name="w1g_%d" % t)
             nc.scalar.activation(w1g[:], gate[:], ACT.Identity, scale=neg_gain[:, t : t + 1], bias=gain[:, t : t + 1])
             nc.vector.tensor_tensor(from_n3[:, t, :], y[:].indirect(n3_sb[:]), w3[:], ALU.mult)
             nc.vector.tensor_tensor(from_n1[:, t, :], y[:].indirect(n1_sb[:]), w1g[:], ALU.mult)
+            if t == 0:
+                y_tiles.append(keep.tile([P, WINDOW], F32, name="y3", tag="y0"))
+                nc.vector.tensor_copy(y_tiles[PACK - 1][:, 0:S], y_banks[PACK - 2][:])
 
         z_bf = keep.tile([P, S, PACK], BF16, align_bytes=64)
         z_codes = keep.tile([P, S], U32, align_bytes=64)
         z_scales = keep.tile([P, S], U8, align_bytes=64)
-        s_banks = [[psum.tile([P, S // 2], F32, name="s_bank%d" % t, tag="s%d" % t) for t in range(PACK)]]
-        s_banks.append([psum.tile([P, S // 2], F32, name="s_bankb%d" % t, tag="y_bank%d" % t) for t in range(PACK)])
         s_tiles = [keep.tile([P, WINDOW], F32, name="s%d" % t) for t in range(PACK)]
-        for h in range(2):
-            cols = slice(256 * h, 256 * (h + 1))
+        neg_s = [keep.tile([P, S], F32, name="neg_s%d" % t) for t in range(PACK - 1)]
+        pos_s = [keep.tile([P, S], F32, name="pos_s%d" % t) for t in range(PACK - 1)]
+        first_banks = [bank(n, b - a, "s0_bank%d" % n) for n, (a, b) in enumerate(Z_CHUNKS)]
+        s_banks = [bank(4 + t, S, "s_bank%d" % t) for t in range(1, PACK)]
+
+        def blend(a, b):
             nc.vector.tensor_tensor(
-                z_bf[:, cols, :].rearrange("p (c i) t -> p c t i", i=4),
-                from_n1[:, :, cols].rearrange("p t (c i) -> p c t i", i=4),
-                from_n3[:, :, cols].rearrange("p t (c i) -> p c t i", i=4),
+                z_bf[:, a:b, :].rearrange("p (c i) t -> p c t i", i=4),
+                from_n1[:, :, a:b].rearrange("p t (c i) -> p c t i", i=4),
+                from_n3[:, :, a:b].rearrange("p t (c i) -> p c t i", i=4),
                 ALU.add,
             )
-        for h in range(2):
-            cols = slice(256 * h, 256 * (h + 1))
+
+        def score(n):
+            a, b = Z_CHUNKS[n]
             nc.vector.quantize_mx(
-                out=z_codes[:, cols].bitcast(FP8X4),
-                scales=z_scales[:, cols],
-                in_=z_bf[:, cols, :].rearrange("p c t -> p (c t)"),
+                out=z_codes[:, a:b].bitcast(FP8X4),
+                scales=z_scales[:, a:b],
+                in_=z_bf[:, a:b, :].rearrange("p c t -> p (c t)"),
             )
             for t in range(PACK):
                 rows = slice(P * t, P * (t + 1))
                 nc.tensor.matmul_mx(
-                    out=s_banks[h][t][:],
+                    out=first_banks[n][:] if t == 0 else s_banks[t - 1][:, a:b],
                     lhsT=cand_words_dealt[:, rows].bitcast(FP8X4),
                     lhsT_scale=cand_plane[:, rows],
-                    rhs=z_codes[:, cols].bitcast(FP8X4),
-                    rhs_scale=z_scales[:, cols],
+                    rhs=z_codes[:, a:b].bitcast(FP8X4),
+                    rhs_scale=z_scales[:, a:b],
                     start=True,
                     stop=True,
                 )
-            for t in range(PACK):
-                nc.scalar.activation(s_tiles[t][:, cols], s_banks[h][t][:], ACT.Copy, scale=SCORE_SCALE)
+            nc.scalar.activation(s_tiles[0][:, a:b], first_banks[n][:], ACT.Copy, scale=SCORE_SCALE)
+            nc.scalar.activation(pos_s[0][:, a:b], first_banks[n][:], ACT.Copy, scale=SCORE_SCALE)
+            nc.scalar.activation(neg_s[0][:, a:b], first_banks[n][:], ACT.Copy, scale=-SCORE_SCALE)
+
+        for n, (a, b) in enumerate(Z_CHUNKS):
+            blend(a, b)
+            if n > 0:
+                score(n - 1)
+        score(len(Z_CHUNKS) - 1)
+        for t in range(1, PACK):
+            nc.scalar.activation(s_tiles[t][:, 0:S], s_banks[t - 1][:], ACT.Copy, scale=SCORE_SCALE)
+            if t < PACK - 1:
+                nc.scalar.activation(pos_s[t][:], s_banks[t - 1][:], ACT.Copy, scale=SCORE_SCALE)
+                nc.scalar.activation(neg_s[t][:], s_banks[t - 1][:], ACT.Copy, scale=-SCORE_SCALE)
 
         out_rows = out.rearrange("(u t e) c -> t u e c", t=PACK, e=4)
-        for t in range(PACK):
+        for t in range(PACK - 1):
             s = s_tiles[t]
-            at_n5 = keep.tile([P, S], F32, name="at_n5_%d" % t)
-            nc.vector.tensor_copy(at_n5[:], s[:].indirect(n5_sb[:]))
-            diff = keep.tile([P, S], F32, name="diff%d" % t)
-            nc.vector.tensor_tensor(diff[:], s[:].indirect(n4_sb[:]), at_n5[:], ALU.subtract)
+            by_n4 = keep.tile([P, S], F32, name="by_n4_%d" % t)
+            by_n5 = keep.tile([P, S], F32, name="by_n5_%d" % t)
             res = keep.tile([P, S], F32, name="res%d" % t)
-            nc.vector.tensor_tensor(res[:], diff[:], s[:, 0:S], ALU.mult)
+            nc.vector.tensor_tensor(by_n4[:], s[:].indirect(n4_sb[:]), pos_s[t][:], ALU.mult)
+            nc.vector.tensor_tensor(by_n5[:], s[:].indirect(n5_sb[:]), neg_s[t][:], ALU.mult)
+            for h in range(2):
+                turned = bank(3 + h, 256, "turned%d_%d" % (t, h))
+                for i in range(2):
+                    cols = slice(256 * h + P * i, 256 * h + P * (i + 1))
+                    blk = slice(P * i, P * (i + 1))
+                    nc.tensor.matmul(turned[:, blk], by_n4[:, cols], ident[:], start=True, stop=False, is_transpose=True)
+                    nc.tensor.matmul(turned[:, blk], by_n5[:, cols], ident[:], start=False, stop=True, is_transpose=True)
+                turned_sb = keep.tile([P, 256], F32, name="turned_sb%d_%d" % (t, h))
+                nc.scalar.copy(turned_sb[:], turned[:])
+                back = bank(h, 256, "back%d_%d" % (t, h))
+                for i in range(2):
+                    blk = slice(P * i, P * (i + 1))
+                    nc.tensor.transpose(back[:, blk], turned_sb[:, blk], ident[:])
+                nc.scalar.copy(res[:, 256 * h : 256 * (h + 1)], back[:])
             nc.sync.dma_start(out_rows[t], res[:])
+
+        t = PACK - 1
+        s = s_tiles[t]
+        at_n5 = keep.tile([P, S], F32)
+        diff = keep.tile([P, S], F32)
+        last = keep.tile([P, S], F32)
+        nc.vector.tensor_copy(at_n5[:], s[:].indirect(n5_sb[:]))
+        for h in range(2):
+            cols = slice(256 * h, 256 * (h + 1))
+            nc.vector.tensor_tensor(diff[:, cols], s[:].indirect(n4_sb[:, 16 * h : 16 * (h + 1)]), at_n5[:, cols], ALU.subtract)
+        for h in range(2):
+            cols = slice(256 * h, 256 * (h + 1))
+            nc.vector.tensor_tensor(last[:, cols], diff[:, cols], s[:, cols], ALU.mult)
+            nc.sync.dma_start(out_rows[t][:, :, cols], last[:, cols])

@@ -20,7 +20,7 @@ P = 128
 PACK = 4
 WINDOW = 1024
 SCORE_SCALE = 0.0625
-Z_CHUNKS = [(0, 256), (256, 384), (384, 512)]
+Z_CHUNKS = [(0, 128), (256, 512), (128, 256)]
 
 
 def tile_picked_hcandlerpwind_none_p_kernel(
@@ -130,80 +130,120 @@ def tile_picked_hcandlerpwind_none_p_kernel(
 
         cand_words = keep.tile([P, C], U32, align_bytes=64)
         nc.vector.tensor_copy(cand_words[:], table_words[:].indirect(cand_sb[:]))
-        cand_words_dealt = keep.tile([P, C], U32, align_bytes=64)
+        by_tile = cand_words[:].rearrange("p (u t e) -> p t u e", t=PACK, e=4)
+        cand_first = keep.tile([P, P], U32, align_bytes=64)
         nc.vector.tensor_copy(
-            cand_words_dealt[:].rearrange("p (t u e) -> p u t e", t=PACK, e=4),
-            cand_words[:].rearrange("p (u t e) -> p u t e", t=PACK, e=4),
+            cand_first[:].rearrange("p (u e) -> p u e", e=4),
+            by_tile[:, 0, :, :],
         )
 
-        y_tiles = [keep.tile([P, WINDOW], F32, name="y%d" % t) for t in range(PACK - 1)]
+        y_tiles = [keep.tile([P, WINDOW], F32, name="y%d" % t) for t in range(PACK)]
         for h in range(2):
             nc.scalar.copy(y_tiles[0][:, 256 * h : 256 * (h + 1)], y0_banks[h][:])
-        for t in range(1, PACK - 1):
+        for t in range(1, PACK):
             nc.vector.tensor_copy(y_tiles[t][:, 0:S], y_banks[t - 1][:])
         from_n1 = keep.tile([P, PACK, S], F32)
         from_n3 = keep.tile([P, PACK, S], F32)
+        sum_banks = [psum.tile([P, PACK, P], F32, name="sum_bank%d" % b, tag="bank%d" % (4 + b)) for b in range(2)]
         for t in range(PACK):
             y = y_tiles[t]
             gate = keep.tile([P, S], F32, name="gate%d" % t)
             for h in range(2):
                 nc.scalar.activation(gate[:, 256 * h : 256 * (h + 1)], y[:].indirect(n2_sb[:, 16 * h : 16 * (h + 1)]), ACT.Sigmoid)
             w3 = keep.tile([P, S], F32, name="w3_%d" % t)
-            for h in range(2):
-                cols = slice(256 * h, 256 * (h + 1))
-                nc.scalar.activation(w3[:, cols], gate[:, cols], ACT.Copy, scale=gain[:, t : t + 1])
             w1g = keep.tile([P, S], F32, name="w1g_%d" % t)
-            nc.scalar.activation(w1g[:], gate[:], ACT.Identity, scale=neg_gain[:, t : t + 1], bias=gain[:, t : t + 1])
-            nc.vector.tensor_tensor(from_n3[:, t, :], y[:].indirect(n3_sb[:]), w3[:], ALU.mult)
-            nc.vector.tensor_tensor(from_n1[:, t, :], y[:].indirect(n1_sb[:]), w1g[:], ALU.mult)
-            if t == 0:
-                y_tiles.append(keep.tile([P, WINDOW], F32, name="y3", tag="y0"))
-                nc.vector.tensor_copy(y_tiles[PACK - 1][:, 0:S], y_banks[PACK - 2][:])
+            if t == PACK - 1:
+                for h in range(2):
+                    cols = slice(256 * h, 256 * (h + 1))
+                    ent = slice(16 * h, 16 * (h + 1))
+                    nc.scalar.activation(w3[:, cols], gate[:, cols], ACT.Copy, scale=gain[:, t : t + 1])
+                    nc.scalar.activation(
+                        w1g[:, cols], gate[:, cols], ACT.Identity, scale=neg_gain[:, t : t + 1], bias=gain[:, t : t + 1]
+                    )
+                    nc.vector.tensor_tensor(from_n3[:, t, cols], y[:].indirect(n3_sb[:, ent]), w3[:, cols], ALU.mult)
+                    nc.vector.tensor_tensor(from_n1[:, t, cols], y[:].indirect(n1_sb[:, ent]), w1g[:, cols], ALU.mult)
+            else:
+                for h in range(2):
+                    cols = slice(256 * h, 256 * (h + 1))
+                    nc.scalar.activation(w3[:, cols], gate[:, cols], ACT.Copy, scale=gain[:, t : t + 1])
+                nc.scalar.activation(w1g[:], gate[:], ACT.Identity, scale=neg_gain[:, t : t + 1], bias=gain[:, t : t + 1])
+                nc.vector.tensor_tensor(from_n3[:, t, :], y[:].indirect(n3_sb[:]), w3[:], ALU.mult)
+                nc.vector.tensor_tensor(from_n1[:, t, :], y[:].indirect(n1_sb[:]), w1g[:], ALU.mult)
+            for src, first in ((from_n3, True), (from_n1, False)):
+                for b in range(2):
+                    nc.tensor.matmul(
+                        sum_banks[b][:, t, :],
+                        src[:, t, P * b : P * (b + 1)],
+                        ident[:],
+                        start=first,
+                        stop=not first,
+                        is_transpose=True,
+                    )
 
-        z_bf = keep.tile([P, S, PACK], BF16, align_bytes=64)
+        z_bf = [keep.tile([P, b - a, PACK], BF16, name="z_bf%d" % a, align_bytes=64) for a, b in Z_CHUNKS]
         z_codes = keep.tile([P, S], U32, align_bytes=64)
         z_scales = keep.tile([P, S], U8, align_bytes=64)
         s_tiles = [keep.tile([P, WINDOW], F32, name="s%d" % t) for t in range(PACK)]
         neg_s = [keep.tile([P, S], F32, name="neg_s%d" % t) for t in range(PACK - 1)]
         pos_s = [keep.tile([P, S], F32, name="pos_s%d" % t) for t in range(PACK - 1)]
-        first_banks = [bank(n, b - a, "s0_bank%d" % n) for n, (a, b) in enumerate(Z_CHUNKS)]
-        s_banks = [bank(4 + t, S, "s_bank%d" % t) for t in range(1, PACK)]
 
-        def blend(a, b):
-            nc.vector.tensor_tensor(
-                z_bf[:, a:b, :].rearrange("p (c i) t -> p c t i", i=4),
-                from_n1[:, :, a:b].rearrange("p t (c i) -> p c t i", i=4),
-                from_n3[:, :, a:b].rearrange("p t (c i) -> p c t i", i=4),
-                ALU.add,
+        z_turned = [keep.tile([P, P, PACK], BF16, name="z_turned%d" % b) for b in range(2)]
+        for b in range(2):
+            nc.scalar.copy(z_turned[b][:], sum_banks[b][:].rearrange("c t p -> c p t"))
+        for b in range(2):
+            pairs = z_turned[b][:].rearrange("c p t -> c (p t)").bitcast(F32)
+            z_back = psum.tile([P, 2, P], F32, name="z_back%d" % b, tag="bank%d" % (1 + b))
+            for u in range(2):
+                nc.tensor.transpose(z_back[:, u, :], pairs[:, u : 2 * P : 2], ident[:])
+            nc.scalar.copy(
+                z_bf[2 * b][:].rearrange("p c t -> p (c t)").bitcast(F32).rearrange("p (c u) -> p c u", u=2),
+                z_back[:].rearrange("p u c -> p c u"),
+            )
+        nc.vector.tensor_tensor(
+            z_bf[1][:].rearrange("p (c i) t -> p c t i", i=4),
+            from_n1[:, :, 256:S].rearrange("p t (c i) -> p c t i", i=4),
+            from_n3[:, :, 256:S].rearrange("p t (c i) -> p c t i", i=4),
+            ALU.add,
+        )
+
+        first_banks = [bank(n, b - a, "s0_bank%d" % n) for n, (a, b) in enumerate(Z_CHUNKS)]
+        s_banks = [bank(number, S, "s_bank%d" % number) for number in (3, 6, 7)]
+
+        def score(dst, words, t, a, b):
+            nc.tensor.matmul_mx(
+                out=dst,
+                lhsT=words.bitcast(FP8X4),
+                lhsT_scale=cand_plane[:, P * t : P * (t + 1)],
+                rhs=z_codes[:, a:b].bitcast(FP8X4),
+                rhs_scale=z_scales[:, a:b],
+                start=True,
+                stop=True,
             )
 
-        def score(n):
-            a, b = Z_CHUNKS[n]
+        for n, (a, b) in enumerate(Z_CHUNKS):
             nc.vector.quantize_mx(
                 out=z_codes[:, a:b].bitcast(FP8X4),
                 scales=z_scales[:, a:b],
-                in_=z_bf[:, a:b, :].rearrange("p c t -> p (c t)"),
+                in_=z_bf[n][:].rearrange("p c t -> p (c t)"),
             )
-            for t in range(PACK):
-                rows = slice(P * t, P * (t + 1))
-                nc.tensor.matmul_mx(
-                    out=first_banks[n][:] if t == 0 else s_banks[t - 1][:, a:b],
-                    lhsT=cand_words_dealt[:, rows].bitcast(FP8X4),
-                    lhsT_scale=cand_plane[:, rows],
-                    rhs=z_codes[:, a:b].bitcast(FP8X4),
-                    rhs_scale=z_scales[:, a:b],
-                    start=True,
-                    stop=True,
-                )
-            nc.scalar.activation(s_tiles[0][:, a:b], first_banks[n][:], ACT.Copy, scale=SCORE_SCALE)
-            nc.scalar.activation(pos_s[0][:, a:b], first_banks[n][:], ACT.Copy, scale=SCORE_SCALE)
-            nc.scalar.activation(neg_s[0][:, a:b], first_banks[n][:], ACT.Copy, scale=-SCORE_SCALE)
-
+            score(first_banks[n][:], cand_first[:], 0, a, b)
+        cand_rest = keep.tile([P, (PACK - 1) * P], U32, tag="z_bf128", align_bytes=64)
+        nc.vector.tensor_copy(
+            cand_rest[:].rearrange("p (t u e) -> p u t e", t=PACK - 1, e=4),
+            cand_words[:].rearrange("p (u t e) -> p u t e", t=PACK, e=4)[:, :, 1:PACK, :],
+        )
         for n, (a, b) in enumerate(Z_CHUNKS):
-            blend(a, b)
-            if n > 0:
-                score(n - 1)
-        score(len(Z_CHUNKS) - 1)
+            if n < len(Z_CHUNKS) - 1:
+                nc.scalar.activation(s_tiles[0][:, a:b], first_banks[n][:], ACT.Copy, scale=SCORE_SCALE)
+            else:
+                nc.vector.tensor_scalar(s_tiles[0][:, a:b], first_banks[n][:], SCORE_SCALE, None, ALU.mult)
+        for n in (1, 0, 2):
+            a, b = Z_CHUNKS[n]
+            nc.scalar.activation(pos_s[0][:, a:b], first_banks[n][:], ACT.Copy, scale=SCORE_SCALE)
+        for n, (a, b) in enumerate(Z_CHUNKS):
+            nc.scalar.activation(neg_s[0][:, a:b], first_banks[n][:], ACT.Copy, scale=-SCORE_SCALE)
+        for t in range(1, PACK):
+            score(s_banks[t - 1][:], cand_rest[:, P * (t - 1) : P * t], t, 0, S)
         for t in range(1, PACK):
             nc.scalar.activation(s_tiles[t][:, 0:S], s_banks[t - 1][:], ACT.Copy, scale=SCORE_SCALE)
             if t < PACK - 1:
@@ -216,10 +256,20 @@ def tile_picked_hcandlerpwind_none_p_kernel(
             by_n4 = keep.tile([P, S], F32, name="by_n4_%d" % t)
             by_n5 = keep.tile([P, S], F32, name="by_n5_%d" % t)
             res = keep.tile([P, S], F32, name="res%d" % t)
-            nc.vector.tensor_tensor(by_n4[:], s[:].indirect(n4_sb[:]), pos_s[t][:], ALU.mult)
-            nc.vector.tensor_tensor(by_n5[:], s[:].indirect(n5_sb[:]), neg_s[t][:], ALU.mult)
+            if t > 0:
+                nc.vector.tensor_tensor(by_n4[:], s[:].indirect(n4_sb[:]), pos_s[t][:], ALU.mult)
+            else:
+                for h in (1, 0):
+                    cols = slice(256 * h, 256 * (h + 1))
+                    nc.vector.tensor_tensor(by_n4[:, cols], s[:].indirect(n4_sb[:, 16 * h : 16 * (h + 1)]), pos_s[t][:, cols], ALU.mult)
+            if t < PACK - 2:
+                nc.vector.tensor_tensor(by_n5[:], s[:].indirect(n5_sb[:]), neg_s[t][:], ALU.mult)
+            else:
+                for h in range(2):
+                    cols = slice(256 * h, 256 * (h + 1))
+                    nc.vector.tensor_tensor(by_n5[:, cols], s[:].indirect(n5_sb[:, 16 * h : 16 * (h + 1)]), neg_s[t][:, cols], ALU.mult)
             for h in range(2):
-                turned = bank(3 + h, 256, "turned%d_%d" % (t, h))
+                turned = bank(4 + h, 256, "turned%d_%d" % (t, h))
                 for i in range(2):
                     cols = slice(256 * h + P * i, 256 * h + P * (i + 1))
                     blk = slice(P * i, P * (i + 1))
@@ -232,7 +282,7 @@ def tile_picked_hcandlerpwind_none_p_kernel(
                     blk = slice(P * i, P * (i + 1))
                     nc.tensor.transpose(back[:, blk], turned_sb[:, blk], ident[:])
                 nc.scalar.copy(res[:, 256 * h : 256 * (h + 1)], back[:])
-            nc.sync.dma_start(out_rows[t], res[:])
+                nc.scalar.dma_start(out_rows[t][:, :, 256 * h : 256 * (h + 1)], res[:, 256 * h : 256 * (h + 1)])
 
         t = PACK - 1
         s = s_tiles[t]

@@ -144,31 +144,26 @@ def tile_picked_hcandlerpwind_none_p_kernel(
             nc.vector.tensor_copy(y_tiles[t][:, 0:S], y_banks[t - 1][:])
         from_n1 = keep.tile([P, PACK, S], F32)
         from_n3 = keep.tile([P, PACK, S], F32)
+        gate = keep.tile([P, PACK, S], F32)
+        weight_n3 = keep.tile([P, PACK, S], F32)
+        weight_n1 = keep.tile([P, PACK, S], F32)
         sum_banks = [psum.tile([P, PACK, P], F32, name="sum_bank%d" % b, tag="bank%d" % (4 + b)) for b in range(2)]
-        for t in range(PACK):
-            y = y_tiles[t]
-            gate = keep.tile([P, S], F32, name="gate%d" % t)
-            for h in range(2):
-                nc.scalar.activation(gate[:, 256 * h : 256 * (h + 1)], y[:].indirect(n2_sb[:, 16 * h : 16 * (h + 1)]), ACT.Sigmoid)
-            w3 = keep.tile([P, S], F32, name="w3_%d" % t)
-            w1g = keep.tile([P, S], F32, name="w1g_%d" % t)
-            if t == PACK - 1:
-                for h in range(2):
-                    cols = slice(256 * h, 256 * (h + 1))
-                    ent = slice(16 * h, 16 * (h + 1))
-                    nc.scalar.activation(w3[:, cols], gate[:, cols], ACT.Copy, scale=gain[:, t : t + 1])
-                    nc.scalar.activation(
-                        w1g[:, cols], gate[:, cols], ACT.Identity, scale=neg_gain[:, t : t + 1], bias=gain[:, t : t + 1]
-                    )
-                    nc.vector.tensor_tensor(from_n3[:, t, cols], y[:].indirect(n3_sb[:, ent]), w3[:, cols], ALU.mult)
-                    nc.vector.tensor_tensor(from_n1[:, t, cols], y[:].indirect(n1_sb[:, ent]), w1g[:, cols], ALU.mult)
-            else:
-                for h in range(2):
-                    cols = slice(256 * h, 256 * (h + 1))
-                    nc.scalar.activation(w3[:, cols], gate[:, cols], ACT.Copy, scale=gain[:, t : t + 1])
-                nc.scalar.activation(w1g[:], gate[:], ACT.Identity, scale=neg_gain[:, t : t + 1], bias=gain[:, t : t + 1])
-                nc.vector.tensor_tensor(from_n3[:, t, :], y[:].indirect(n3_sb[:]), w3[:], ALU.mult)
-                nc.vector.tensor_tensor(from_n1[:, t, :], y[:].indirect(n1_sb[:]), w1g[:], ALU.mult)
+
+        def gates(t, a, b):
+            nc.scalar.activation(gate[:, t, a:b], y_tiles[t][:].indirect(n2_sb[:, a // 16 : b // 16]), ACT.Sigmoid)
+
+        def weigh_n3(t, a, b):
+            nc.scalar.activation(weight_n3[:, t, a:b], gate[:, t, a:b], ACT.Copy, scale=gain[:, t : t + 1])
+
+        def weigh_n1(t, a, b):
+            nc.scalar.activation(
+                weight_n1[:, t, a:b], gate[:, t, a:b], ACT.Identity, scale=neg_gain[:, t : t + 1], bias=gain[:, t : t + 1]
+            )
+
+        def fetch(dst, offsets, weight, t, a, b):
+            nc.vector.tensor_tensor(dst[:, t, a:b], y_tiles[t][:].indirect(offsets[:, a // 16 : b // 16]), weight[:, t, a:b], ALU.mult)
+
+        def add_turned(t):
             for src, first in ((from_n3, True), (from_n1, False)):
                 for b in range(2):
                     nc.tensor.matmul(
@@ -179,6 +174,26 @@ def tile_picked_hcandlerpwind_none_p_kernel(
                         stop=not first,
                         is_transpose=True,
                     )
+
+        LOW, HIGH = (0, 256), (256, S)
+        for pieces in ([(0, LOW), (0, HIGH)], [(1, LOW), (1, HIGH)], [(2, LOW), (3, LOW)], [(2, HIGH), (3, HIGH)]):
+            for t, (a, b) in pieces:
+                gates(t, a, b)
+            if pieces[0][0] == 1:
+                for t, (a, b) in pieces:
+                    weigh_n3(t, a, b)
+                weigh_n1(1, 0, S)
+                fetch(from_n3, n3_sb, weight_n3, 1, 0, S)
+                fetch(from_n1, n1_sb, weight_n1, 1, 0, S)
+                add_turned(1)
+                continue
+            for t, (a, b) in pieces:
+                weigh_n3(t, a, b)
+                weigh_n1(t, a, b)
+                fetch(from_n3, n3_sb, weight_n3, t, a, b)
+                fetch(from_n1, n1_sb, weight_n1, t, a, b)
+                if a == 0:
+                    add_turned(t)
 
         z_bf = [keep.tile([P, b - a, PACK], BF16, name="z_bf%d" % a, align_bytes=64) for a, b in Z_CHUNKS]
         z_codes = keep.tile([P, S], U32, align_bytes=64)

from contextlib import ExitStack

import concourse.mybir as mybir
from concourse.masks import make_identity

K, T, S, H, C = 512, 2048, 512, 512, 512
FLOPS = 2 * K * H * S + 2 * H * C * S

F32 = mybir.dt.float32
BF16 = mybir.dt.bfloat16
I32 = mybir.dt.int32
U32 = mybir.dt.uint32
U16 = mybir.dt.uint16
U8 = mybir.dt.uint8
FP8X4 = mybir.dt.float8_e4m3fn_x4
ALU = mybir.AluOpType
ACT = mybir.ActivationFunctionType

P = 128
PACK = 4
WINDOW = 1024
SCORE_SCALE = 0.0625
Z_CHUNKS = [(0, 128), (256, 512), (128, 256)]


def tile_picked_hcandlerpwind_none_p_kernel(
    tc, x_words, x_scales, w1, gs, offs, n1, n2, n3, cand, n4, n5, out
):
    nc = tc.nc
    with ExitStack() as ctx:
        lists = ctx.enter_context(tc.tile_pool(name="lists", bufs=1))
        keep = ctx.enter_context(tc.tile_pool(name="keep", bufs=1))
        psum = ctx.enter_context(tc.psum_pool(name="psum", bufs=1))

        def load_list(name, dram):
            offsets = lists.tile([P, S // 16], U16, name=name)
            nc.sync.dma_start(offsets[:], dram)
            return offsets

        def bank(number, width, name):
            return psum.tile([P, width], F32, name=name, tag="bank%d" % number)

        table_scales = keep.tile([P, T], U8, align_bytes=64)
        nc.gpsimd.memset(table_scales[:].bitcast(I32), 0)
        place_plane = keep.tile([P, S], U8, align_bytes=64)
        cand_plane = keep.tile([P, C], U8, align_bytes=64)
        nc.gpsimd.memset(place_plane[:].bitcast(I32), 0)
        nc.gpsimd.memset(cand_plane[:].bitcast(I32), 0)

        offs_sb = load_list("offs_sb", offs)
        nc.sync.dma_start(table_scales[0:P:8, :].bitcast(I32), x_scales[0].bitcast(I32))
        w_rows = w1.rearrange("(p j) c -> p j c", j=PACK)
        half = H // 2
        w_raw = [keep.tile([P, PACK, half], F32, name="w_raw%d" % h) for h in range(2)]
        for h in range(2):
            nc.sync.dma_start(w_raw[h][:], w_rows[:, :, half * h : half * (h + 1)])
        cand_sb = load_list("cand_sb", cand)
        n2_sb = load_list("n2_sb", n2)
        n3_sb = load_list("n3_sb", n3)
        n1_sb = load_list("n1_sb", n1)
        table_words = keep.tile([P, T], U32, align_bytes=64)
        nc.sync.dma_start(table_words[:].bitcast(I32), x_words[0].rearrange("p c r -> p (c r)").bitcast(I32))
        n4_sb = load_list("n4_sb", n4)
        n5_sb = load_list("n5_sb", n5)
        gain = keep.tile([P, PACK], F32)
        nc.gpsimd.dma_start(gain[:], gs.rearrange("(p t) o -> p (t o)", t=PACK))
        neg_gain = keep.tile([P, PACK], F32)
        nc.gpsimd.tensor_scalar(neg_gain[:], gain[:], -1.0, 0.0, ALU.mult, ALU.add)

        warm = keep.tile([P, 1], F32)
        nc.vector.memset(warm[:], 0.0)
        warm_out = keep.tile([P, 1], F32)
        nc.scalar.activation(warm_out[:], warm[:], ACT.Sigmoid)
        ident = keep.tile([P, P], F32)
        make_identity(nc, ident[:])

        def move_scale_rows(plane, picked):
            for j in range(4):
                nc.sync.dma_start(plane[j:P:32, :].bitcast(I32), picked[8 * j : P : 32, :].bitcast(I32))

        place_bytes = keep.tile([P, S], U8, align_bytes=64)
        nc.vector.tensor_copy(place_bytes[:], table_scales[:].indirect(offs_sb[:]))
        move_scale_rows(place_plane, place_bytes)

        w_bf = keep.tile([P, PACK, P, PACK], BF16, align_bytes=64)
        for h in range(2):
            nc.scalar.copy(
                w_bf[:, :, 64 * h : 64 * (h + 1), :].rearrange("p t m j -> p m j t"),
                w_raw[h][:].rearrange("p j (m t) -> p m j t", t=PACK),
            )

        cand_bytes = keep.tile([P, C], U8, align_bytes=64)
        nc.vector.tensor_copy(cand_bytes[:], table_scales[:].indirect(cand_sb[:]))
        cand_bytes_dealt = keep.tile([P, C], U8, align_bytes=64)
        nc.vector.tensor_copy(
            cand_bytes_dealt[:].bitcast(I32).rearrange("p (t u) -> p u t", t=PACK),
            cand_bytes[:].bitcast(I32).rearrange("p (u t) -> p u t", t=PACK),
        )
        move_scale_rows(cand_plane, cand_bytes_dealt)

        w_codes = keep.tile([P, H], U32, align_bytes=64)
        w_scales = keep.tile([P, H], U8, align_bytes=64)
        nc.vector.quantize_mx(
            out=w_codes[:].bitcast(FP8X4), scales=w_scales[:], in_=w_bf[:].rearrange("p t m j -> p (t m j)")
        )
        place_words = keep.tile([P, S], U32, align_bytes=64)
        for h in range(2):
            nc.vector.tensor_copy(
                place_words[:, 256 * h : 256 * (h + 1)], table_words[:].indirect(offs_sb[:, 16 * h : 16 * (h + 1)])
            )

        def project(dst, t, cols):
            rows = slice(P * t, P * (t + 1))
            nc.tensor.matmul_mx(
                out=dst,
                lhsT=w_codes[:, rows].bitcast(FP8X4),
                lhsT_scale=w_scales[:, rows],
                rhs=place_words[:, cols].bitcast(FP8X4),
                rhs_scale=place_plane[:, cols],
                start=True,
                stop=True,
            )

        y0_banks = [bank(4 * h, 256, "y0_bank%d" % h) for h in range(2)]
        for h in range(2):
            project(y0_banks[h][:], 0, slice(256 * h, 256 * (h + 1)))
        y_banks = [bank(t, S, "y_bank%d" % t) for t in range(1, PACK)]
        for t in range(1, PACK):
            project(y_banks[t - 1][:], t, slice(0, S))

        cand_words = keep.tile([P, C], U32, align_bytes=64)
        nc.vector.tensor_copy(cand_words[:], table_words[:].indirect(cand_sb[:]))
        by_tile = cand_words[:].rearrange("p (u t e) -> p t u e", t=PACK, e=4)
        cand_first = keep.tile([P, P], U32, align_bytes=64)
        nc.vector.tensor_copy(
            cand_first[:].rearrange("p (u e) -> p u e", e=4),
            by_tile[:, 0, :, :],
        )

        y_tiles = [keep.tile([P, WINDOW], F32, name="y%d" % t) for t in range(PACK)]
        for h in range(2):
            nc.scalar.copy(y_tiles[0][:, 256 * h : 256 * (h + 1)], y0_banks[h][:])
        for t in range(1, PACK):
            nc.vector.tensor_copy(y_tiles[t][:, 0:S], y_banks[t - 1][:])
        from_n1 = keep.tile([P, PACK, S], F32)
        from_n3 = keep.tile([P, PACK, S], F32)
        gate = keep.tile([P, PACK, S], F32)
        weight_n3 = keep.tile([P, PACK, S], F32)
        weight_n1 = keep.tile([P, PACK, S], F32)
        sum_banks = [psum.tile([P, PACK, P], F32, name="sum_bank%d" % b, tag="bank%d" % (4 + b)) for b in range(2)]

        def gates(t, a, b):
            nc.scalar.activation(gate[:, t, a:b], y_tiles[t][:].indirect(n2_sb[:, a // 16 : b // 16]), ACT.Sigmoid)

        def weigh_n3(t, a, b):
            nc.scalar.activation(weight_n3[:, t, a:b], gate[:, t, a:b], ACT.Copy, scale=gain[:, t : t + 1])

        def weigh_n1(t, a, b):
            nc.scalar.activation(
                weight_n1[:, t, a:b], gate[:, t, a:b], ACT.Identity, scale=neg_gain[:, t : t + 1], bias=gain[:, t : t + 1]
            )

        def fetch(dst, offsets, weight, t, a, b):
            nc.vector.tensor_tensor(dst[:, t, a:b], y_tiles[t][:].indirect(offsets[:, a // 16 : b // 16]), weight[:, t, a:b], ALU.mult)

        def add_turned(t):
            for src, first in ((from_n3, True), (from_n1, False)):
                for b in range(2):
                    nc.tensor.matmul(
                        sum_banks[b][:, t, :],
                        src[:, t, P * b : P * (b + 1)],
                        ident[:],
                        start=first,
                        stop=not first,
                        is_transpose=True,
                    )

        LOW, HIGH = (0, 256), (256, S)
        for pieces in ([(0, LOW), (0, HIGH)], [(1, LOW), (1, HIGH)], [(2, LOW), (3, LOW)], [(2, HIGH), (3, HIGH)]):
            for t, (a, b) in pieces:
                gates(t, a, b)
            if pieces[0][0] == 1:
                for t, (a, b) in pieces:
                    weigh_n3(t, a, b)
                weigh_n1(1, 0, S)
                fetch(from_n3, n3_sb, weight_n3, 1, 0, S)
                fetch(from_n1, n1_sb, weight_n1, 1, 0, S)
                add_turned(1)
                continue
            for t, (a, b) in pieces:
                weigh_n3(t, a, b)
                weigh_n1(t, a, b)
                fetch(from_n3, n3_sb, weight_n3, t, a, b)
                fetch(from_n1, n1_sb, weight_n1, t, a, b)
                if a == 0:
                    add_turned(t)

        z_bf = [keep.tile([P, b - a, PACK], BF16, name="z_bf%d" % a, align_bytes=64) for a, b in Z_CHUNKS]
        z_codes = keep.tile([P, S], U32, align_bytes=64)
        z_scales = keep.tile([P, S], U8, align_bytes=64)
        s_tiles = [keep.tile([P, WINDOW], F32, name="s%d" % t) for t in range(PACK)]
        neg_s = [keep.tile([P, S], F32, name="neg_s%d" % t) for t in range(PACK - 1)]
        pos_s = [keep.tile([P, S], F32, name="pos_s%d" % t) for t in range(PACK - 1)]

        z_turned = [keep.tile([P, P, PACK], BF16, name="z_turned%d" % b) for b in range(2)]
        for b in range(2):
            nc.scalar.copy(z_turned[b][:], sum_banks[b][:].rearrange("c t p -> c p t"))
        for b in range(2):
            pairs = z_turned[b][:].rearrange("c p t -> c (p t)").bitcast(F32)
            z_back = psum.tile([P, 2, P], F32, name="z_back%d" % b, tag="bank%d" % (1 + b))
            for u in range(2):
                nc.tensor.transpose(z_back[:, u, :], pairs[:, u : 2 * P : 2], ident[:])
            nc.scalar.copy(
                z_bf[2 * b][:].rearrange("p c t -> p (c t)").bitcast(F32).rearrange("p (c u) -> p c u", u=2),
                z_back[:].rearrange("p u c -> p c u"),
            )
        nc.vector.tensor_tensor(
            z_bf[1][:].rearrange("p (c i) t -> p c t i", i=4),
            from_n1[:, :, 256:S].rearrange("p t (c i) -> p c t i", i=4),
            from_n3[:, :, 256:S].rearrange("p t (c i) -> p c t i", i=4),
            ALU.add,
        )

        first_banks = [bank(n, b - a, "s0_bank%d" % n) for n, (a, b) in enumerate(Z_CHUNKS)]
        s_banks = [bank(number, S, "s_bank%d" % number) for number in (3, 6, 7)]

        def score(dst, words, t, a, b):
            nc.tensor.matmul_mx(
                out=dst,
                lhsT=words.bitcast(FP8X4),
                lhsT_scale=cand_plane[:, P * t : P * (t + 1)],
                rhs=z_codes[:, a:b].bitcast(FP8X4),
                rhs_scale=z_scales[:, a:b],
                start=True,
                stop=True,
            )

        for n, (a, b) in enumerate(Z_CHUNKS):
            nc.vector.quantize_mx(
                out=z_codes[:, a:b].bitcast(FP8X4),
                scales=z_scales[:, a:b],
                in_=z_bf[n][:].rearrange("p c t -> p (c t)"),
            )
            score(first_banks[n][:], cand_first[:], 0, a, b)
        cand_rest = keep.tile([P, (PACK - 1) * P], U32, tag="z_bf128", align_bytes=64)
        nc.vector.tensor_copy(
            cand_rest[:].rearrange("p (t u e) -> p u t e", t=PACK - 1, e=4),
            cand_words[:].rearrange("p (u t e) -> p u t e", t=PACK, e=4)[:, :, 1:PACK, :],
        )
        for n, (a, b) in enumerate(Z_CHUNKS):
            if n < len(Z_CHUNKS) - 1:
                nc.scalar.activation(s_tiles[0][:, a:b], first_banks[n][:], ACT.Copy, scale=SCORE_SCALE)
            else:
                nc.vector.tensor_scalar(s_tiles[0][:, a:b], first_banks[n][:], SCORE_SCALE, None, ALU.mult)
        for n in (1, 0, 2):
            a, b = Z_CHUNKS[n]
            nc.scalar.activation(pos_s[0][:, a:b], first_banks[n][:], ACT.Copy, scale=SCORE_SCALE)
        for n, (a, b) in enumerate(Z_CHUNKS):
            nc.scalar.activation(neg_s[0][:, a:b], first_banks[n][:], ACT.Copy, scale=-SCORE_SCALE)
        for t in range(1, PACK):
            score(s_banks[t - 1][:], cand_rest[:, P * (t - 1) : P * t], t, 0, S)
        for t in range(1, PACK):
            nc.scalar.activation(s_tiles[t][:, 0:S], s_banks[t - 1][:], ACT.Copy, scale=SCORE_SCALE)
            if t < PACK - 1:
                nc.scalar.activation(pos_s[t][:], s_banks[t - 1][:], ACT.Copy, scale=SCORE_SCALE)
                nc.scalar.activation(neg_s[t][:], s_banks[t - 1][:], ACT.Copy, scale=-SCORE_SCALE)

        out_rows = out.rearrange("(u t e) c -> t u e c", t=PACK, e=4)
        for t in range(PACK - 1):
            s = s_tiles[t]
            by_n4 = keep.tile([P, S], F32, name="by_n4_%d" % t)
            by_n5 = keep.tile([P, S], F32, name="by_n5_%d" % t)
            res = keep.tile([P, S], F32, name="res%d" % t)
            if t > 0:
                nc.vector.tensor_tensor(by_n4[:], s[:].indirect(n4_sb[:]), pos_s[t][:], ALU.mult)
            else:
                for h in (1, 0):
                    cols = slice(256 * h, 256 * (h + 1))
                    nc.vector.tensor_tensor(by_n4[:, cols], s[:].indirect(n4_sb[:, 16 * h : 16 * (h + 1)]), pos_s[t][:, cols], ALU.mult)
            if t < PACK - 2:
                nc.vector.tensor_tensor(by_n5[:], s[:].indirect(n5_sb[:]), neg_s[t][:], ALU.mult)
            else:
                for h in range(2):
                    cols = slice(256 * h, 256 * (h + 1))
                    nc.vector.tensor_tensor(by_n5[:, cols], s[:].indirect(n5_sb[:, 16 * h : 16 * (h + 1)]), neg_s[t][:, cols], ALU.mult)
            for h in range(2):
                turned = bank(4 + h, 256, "turned%d_%d" % (t, h))
                for i in range(2):
                    cols = slice(256 * h + P * i, 256 * h + P * (i + 1))
                    blk = slice(P * i, P * (i + 1))
                    nc.tensor.matmul(turned[:, blk], by_n4[:, cols], ident[:], start=True, stop=False, is_transpose=True)
                    nc.tensor.matmul(turned[:, blk], by_n5[:, cols], ident[:], start=False, stop=True, is_transpose=True)
                turned_sb = keep.tile([P, 256], F32, name="turned_sb%d_%d" % (t, h))
                nc.scalar.copy(turned_sb[:], turned[:])
                back = bank(h, 256, "back%d_%d" % (t, h))
                for i in range(2):
                    blk = slice(P * i, P * (i + 1))
                    nc.tensor.transpose(back[:, blk], turned_sb[:, blk], ident[:])
                nc.scalar.copy(res[:, 256 * h : 256 * (h + 1)], back[:])
                nc.scalar.dma_start(out_rows[t][:, :, 256 * h : 256 * (h + 1)], res[:, 256 * h : 256 * (h + 1)])

        t = PACK - 1
        s = s_tiles[t]
        at_n5 = keep.tile([P, S], F32)
        diff = keep.tile([P, S], F32)
        last = keep.tile([P, S], F32)
        nc.vector.tensor_copy(at_n5[:], s[:].indirect(n5_sb[:]))
        for h in range(2):
            cols = slice(256 * h, 256 * (h + 1))
            nc.vector.tensor_tensor(diff[:, cols], s[:].indirect(n4_sb[:, 16 * h : 16 * (h + 1)]), at_n5[:, cols], ALU.subtract)
        for h in range(2):
            cols = slice(256 * h, 256 * (h + 1))
            nc.vector.tensor_tensor(last[:, cols], diff[:, cols], s[:, cols], ALU.mult)
            nc.sync.dma_start(out_rows[t][:, :, cols], last[:, cols])
